import numpy as np, ml_dtypes
CORES = [30,158,46,174,86,214]
N = 6
import mx_ref
BF = ml_dtypes.bfloat16
def f(rng, *shape):
    return mx_ref.flush((rng.standard_normal(shape, dtype=np.float32) * np.exp2(rng.integers(-2, 3, shape[:-1] + (1,)))).astype(BF))
def wide(rng, *shape, cols=0):
    v = rng.standard_normal(shape, dtype=np.float32) * np.exp2(rng.integers(-12, 13, shape)).astype(np.float32)
    if cols: v *= np.repeat(np.exp2(rng.integers(-cols, cols + 1, shape[:-2] + (1, shape[-1] // 4))) * (rng.random(shape[:-2] + (1, shape[-1] // 4)) > 0.0625), 4, axis=-1).astype(np.float32)
    return mx_ref.flush(v.astype(BF))
PG, PW = 8, 64
def bare(d):
    d["sm"][:, :, 4 * PG:] = 0; d["gs"][:, :, 8:] = 0
    return d
def sizes(rng, d):
    for n in ("sm", "gs"): d[n] = mx_ref.flush((d[n].astype(np.float32) * np.exp2(rng.integers(-12, 13, (N, 1, 1))).astype(np.float32)).astype(BF))
    return d
def setup_inputs(rng):
    return bare({"pg": f(rng, N, 128 * PG, 4 * PW), "sm": f(rng, N, 128, 512), "gs": f(rng, N, 128, 512), "qw": f(rng, N, 128, 1024)})
def setup_inputs_ties(rng):
    d = setup_inputs(rng); v = d["sm"].reshape(N, 128, 128, 4).copy()
    for q in range(N):
        k = rng.integers(PG // 4 + 1, PG // 2 + 1); p = rng.permutation(PG)
        v[q][:, p[k:]] = v[q][:, p[np.arange(k, PG) % k]]
    d["sm"] = v.reshape(N, 128, 512)
    d = sizes(rng, d)
    for r in rng.permutation(N)[:2]: d["gs"][r][:, 4:8] = 0
    return d
def setup_inputs_last(rng):
    d = setup_inputs(rng); c = f(rng, 128, 4)
    for r in range(N):
        j = rng.integers(0, 2)
        d["gs"][r][:, 4 * j:4 * j + 4] = c
        d["sm"][r][:, 4 * PG - 4:4 * PG] = (c.astype(np.float32) * 2).astype(BF)
    return d
def setup_inputs_alike(rng):
    d = setup_inputs(rng); d["gs"] = np.stack([d["gs"][0]] * N); return d
def setup_inputs_below(rng):
    d = setup_inputs(rng)
    d["gs"] = np.abs(d["gs"].astype(np.float32)).astype(BF)
    d["sm"] = (-np.abs(d["sm"].astype(np.float32))).astype(BF)
    return bare(sizes(rng, d))
def setup_inputs_spread(rng):
    d = setup_inputs(rng); d["pg"] = wide(rng, N, 128 * PG, 4 * PW); d["sm"] = wide(rng, N, 128, 512); d["gs"] = wide(rng, N, 128, 512)
    return bare(d)
def check_inputs(d):
    b = []
    for r in range(N):
        if d["sm"][r][:, 4 * PG:].astype(np.float32).any(): b.append("sm")
        if d["gs"][r][:, 8:].astype(np.float32).any(): b.append("gs")
    return b
def reference(pg, sm, gs, qw):
    S = [mx_ref.quantize(t) for t in sm]; G = [mx_ref.quantize(t) for t in gs]
    y = np.zeros((N, 128, 2 * N * PW), np.float32); ch = np.zeros((N, 2, N), np.float32)
    for r in range(N):
        W = [mx_ref.quantize(qw[r][:, 512 * j:512 * j + 512]) for j in range(2)]
        for q in range(N):
            score = mx_ref.matmul(S[q], G[r])
            for j in range(2):
                c = int(np.argmax(score[:PG, j]))
                k = PW * (j * N + q)
                y[r][:, k:k + PW] = mx_ref.matmul(W[j], mx_ref.quantize(pg[q][128 * c:128 * c + 128]))
                ch[r, j, q] = c
    return {"y": y, "ch": ch}

@@ -1,0 +1,294 @@
+from concourse.bass import DstId, RemoteDMATransfer
+from concourse.mybir import dt, AluOpType, ActivationFunctionType
+
+U8 = dt.uint8
+COPY = ActivationFunctionType.Copy
+NR = 6
+NO = NR - 1
+NL = NR - 2
+
+SCRATCH = {
+    "gt": ("sbuf", [128, 512], "bfloat16"),
+    "st": ("sbuf", [128, 512], "bfloat16"),
+    "pgt": ("sbuf", [128, 2048], "bfloat16"),
+    "wt": ("sbuf", [128, 1024], "bfloat16"),
+    "gq": ("sbuf", [128, 144], "float8_e4m3fn_x4"),
+    "gp": ("sbuf", [128, 144], "uint8"),
+    "sq": ("sbuf", [128, 128], "float8_e4m3fn_x4"),
+    "sp": ("sbuf", [128, 128], "uint8"),
+    "wq": ("sbuf", [128, 256], "float8_e4m3fn_x4"),
+    "wp": ("sbuf", [128, 256], "uint8"),
+    "pq": ("sbuf", [128, 512], "float8_e4m3fn_x4"),
+    "pp": ("sbuf", [128, 512], "uint8"),
+    "eq": ("sbuf", [128, 512], "float8_e4m3fn_x4"),
+    "ep": ("sbuf", [128, 512], "uint8"),
+    "hb": ("sbuf", [128, 2048], "bfloat16"),
+    "hq": ("sbuf", [128, 512], "float8_e4m3fn_x4"),
+    "hp": ("sbuf", [128, 512], "uint8"),
+    "lq": ("sbuf", [128, 640], "float8_e4m3fn_x4"),
+    "lp": ("sbuf", [128, 640], "uint8"),
+    "ow": ("sbuf", [128, 2048], "float32"),
+    "yb": ("sbuf", [128, 768], "float32"),
+    "sc": ("sbuf", [128, 32], "float32"),
+    "pm": ("sbuf", [128, 8], "float32"),
+    "lt": ("sbuf", [128, 64], "float32"),
+    "zz": ("sbuf", [128, 40], "float32"),
+    "bb": ("sbuf", [128, 64], "float32"),
+    "bt": ("sbuf", [128, 32], "float32"),
+    "ce": ("sbuf", [128, 2], "float32"),
+    "i0": ("sbuf", [128, 16], "int32"),
+    "i1": ("sbuf", [128, 16], "int32"),
+    "i2": ("sbuf", [128, 16], "int32"),
+    "i3": ("sbuf", [128, 16], "float32"),
+    "if256": ("sbuf", [128, 16], "float32"),
+    "if64": ("sbuf", [128, 4], "float32"),
+    "off": ("sbuf", [128, 128], "uint16"),
+    "offo": ("sbuf", [128, 16], "uint16"),
+    "chs": ("sbuf", [128, 12], "float32"),
+    "cho": ("sbuf", [128, 12], "float32"),
+    "chd": ("dram", [640, 2], "float32"),
+    "dd": ("dram", [128, 2], "float32"),
+    "ps": ("psum", [128, 4096], "float32"),
+}
+SEMAPHORES = (["gsl", "sml", "qwl", "pgl", "mg", "ms", "ml", "mz", "ii", "jj", "k2", "k3", "k4", "k5",
+               "cs", "qg", "qs", "qw", "qp", "sc", "v1", "v2", "v3", "v4", "v5",
+               "gsa", "lg", "le", "ea", "lce", "cea", "lpg", "lch", "dch", "cha", "chl", "chv", "chst", "yst"]
+              + [n + "%d" % t for n in ("gv", "gz", "hq") for t in range(NL)]
+              + ["pa%d" % t for t in range(NO)]
+              + [n + "%d%d" % (t, j) for n in ("of", "mm", "cp") for t in range(NL) for j in range(2)]
+              + [n + "%d" % t for n in ("om", "oc", "oo", "oy") for t in range(4)])
+
+
+def rank_program(g, core, T, topo):
+    r = T.rank_of(core)
+    if r is None:
+        return
+    S = T.sem
+    V, A, P, Y = g.vector, g.scalar, g.tensor, g.sync
+    others = [q for q in range(NR) if q != r]
+    slot = lambda q, at: q - (q > at)
+    order = [(r + 1 + t) % NR for t in range(NL)]
+    come = [(r - 1 - t) % NR for t in range(NL)]
+    eto = (r + NO) % NR
+    efrom = (r + 1) % NR
+    eng = lambda d: topo.mask(core, T.cores[d])
+    allmask = eng(others[0])
+    for d in others:
+        allmask &= eng(d)
+    count = bin(allmask).count("1")
+
+    def did(d):
+        rid, pid = topo.addr(T.cores[d], core)
+        return DstId(rid=rid, pnc=pid)
+
+    Y.dma_start(T.gt[:, 0:8], T.gs[:, 0:8]).then_inc(S.gsl, 16)
+    A.dma_start(T.st[:, 0:32], T.sm[:, 0:32]).then_inc(S.sml, 16)
+    for m in range(8):
+        (Y if m % 2 == 0 else A).dma_start(T.pgt[:, 256 * m:256 * m + 256], T.pg[128 * m:128 * m + 128, :]).then_inc(S.pgl, 16)
+    A.dma_start(T.wt[:], T.qw[:]).then_inc(S.qwl, 16)
+
+    g.iota(T.i0[:], [[0, 16]], 0, 1).then_inc(S.ii, 1)
+    g.iota(T.i1[:], [[16, 16]], 0, 0).then_inc(S.jj, 1)
+    V.memset(T.gt[:, 8:512], 0.0).then_inc(S.mg, 1)
+    V.memset(T.st[:, 32:512], 0.0).then_inc(S.ms, 1)
+    V.memset(T.lt[:, 32:64], 0.0).then_inc(S.ml, 1)
+    V.memset(T.zz[:], 0.0).then_inc(S.mz, 1)
+
+    V.wait_ge(S.mg, 1)
+    V.wait_ge(S.gsl, 16)
+    V.quantize_mx(T.gq[:, 16:144], T.gp[:, 16:144], T.gt[:]).then_inc(S.qg, 1)
+    g.wait_ge(S.qg, 1)
+    ids = [did(d) for d in others]
+    at = [6 + 2 * slot(r, d) for d in others]
+    half = [e for e in range(allmask.bit_length()) if allmask >> e & 1]
+    half = [sum(1 << e for e in half[:count // 2]), sum(1 << e for e in half[count // 2:])]
+    g.remote_dma_fused([RemoteDMATransfer(dst_ids=ids, dma_engine_mask=half[0], remote_sem=S.gsa,
+                                          srcs=[T.gq[:, 16:18].bitcast(U8)],
+                                          dsts=[T.gq[:, a:a + 2].bitcast(U8) for a in at])], local_sem=S.lg)
+    g.remote_dma_fused([RemoteDMATransfer(dst_ids=ids, dma_engine_mask=half[1], remote_sem=S.gsa,
+                                          srcs=[T.gp[:, 16:18]],
+                                          dsts=[T.gp[:, a:a + 2] for a in at])], local_sem=S.lg)
+
+    V.wait_ge(S.ii, 1)
+    V.tensor_scalar(T.i2[:], T.i0[:], 15, None, AluOpType.bitwise_and).then_inc(S.k2, 1)
+    V.wait_ge(S.k2, 1)
+    V.wait_ge(S.jj, 1)
+    V.tensor_tensor(T.i3[:], T.i2[:], T.i1[:], AluOpType.add).then_inc(S.k3, 1)
+    V.wait_ge(S.k3, 1)
+    V.tensor_scalar(T.if256[:], T.i3[:], 1.0 / 256, None, AluOpType.mult).then_inc(S.k4, 1)
+    V.tensor_scalar(T.if64[:], T.i3[:, 0:4], 1.0 / 64, None, AluOpType.mult).then_inc(S.k5, 1)
+
+    V.wait_ge(S.ms, 1)
+    V.wait_ge(S.sml, 16)
+    for a in range(1, 4):
+        V.tensor_copy(T.st[:, 128 * a:128 * a + 32], T.st[:, 0:32]).then_inc(S.cs, 1)
+    V.wait_ge(S.cs, 3)
+    V.quantize_mx(T.sq[:], T.sp[:], T.st[:]).then_inc(S.qs, 1)
+    V.wait_ge(S.pgl, 128)
+    V.quantize_mx(T.pq[:], T.pp[:], T.pgt[:]).then_inc(S.qp, 1)
+    V.wait_ge(S.qwl, 16)
+    V.quantize_mx(T.wq[:], T.wp[:], T.wt[:]).then_inc(S.qw, 1)
+
+    rid, pid = topo.addr(T.cores[eto], core)
+    g.wait_ge(S.qp, 1)
+    g.remote_dma(T["eq"][:].bitcast(U8), T.pq[:].bitcast(U8), S.ea, S.le, pid, rid, eng(eto))
+    g.remote_dma(T["ep"][:], T.pp[:], S.ea, S.le, pid, rid, eng(eto))
+
+    P.wait_ge(S.qs, 1)
+    P.wait_ge(S.qg, 1)
+    P.wait_ge(S.gsa, count * NO)
+    P.matmul_mx(T.ps[:, 0:138], T.sq[:], T.sp[:], T.gq[:, 6:144], T.gp[:, 6:144], True, True).then_inc(S.sc, 1)
+
+    V.wait_ge(S.sc, 1)
+    V.transpose(T["sc"][:], T.ps[:, 0:32]).then_inc(S.v1, 1)
+    V.wait_ge(S.v1, 1)
+    V.tensor_tensor_scan(T["pm"][:], T["sc"][:, 0:8], T["sc"][:, 0:8], T["sc"][:, 0:1],
+                         AluOpType.max, AluOpType.max).then_inc(S.v2, 1)
+    V.wait_ge(S.v2, 1)
+    V.tensor_scalar(T["lt"][:, 24:32], T["pm"][:], T["pm"][:, 7:8], None, AluOpType.is_lt).then_inc(S.v3, 1)
+    V.wait_ge(S.ml, 1)
+    V.wait_ge(S.mz, 1)
+    V.wait_ge(S.v3, 1)
+    V.tensor_tensor_scan(T.bb[:, 24:64], T["lt"][:, 24:64], T.zz[:], 0.0,
+                         AluOpType.add, AluOpType.add).then_inc(S.v4, 1)
+    V.wait_ge(S.v4, 1)
+    V.transpose(T.bt[:], T.bb[:, 32:64]).then_inc(S.v5, 1)
+
+    Y.wait_ge(S.v5, 1)
+    Y.dma_start(T.dd[:], T.bt[0:8, 0:32]).then_inc(S.dch, 16)
+    Y.dma_start(T.chs[0:1, 2 * r:2 * r + 2], T.bt[0:1, 10:12]).then_inc(S.chl, 16)
+    g.wait_ge(S.v5, 1)
+    c = 2 * slot(eto, r)
+    g.remote_dma(T.ce[:], T.bt[:, c:c + 2], S.cea, S.lce, pid, rid, eng(eto))
+
+    V.wait_ge(S.k4, 1)
+    V.wait_ge(S.v5, 1)
+    win = T.pgt[:, 0:2048]
+
+    def offsets(t):
+        for j in (1, 0):
+            c = 2 * slot(order[t], r) + j
+            k = 32 * t + 16 * j
+            V.tensor_scalar(T.off[:, k:k + 16], T.if256[:], T.bt[:, c:c + 1], 256.0,
+                            AluOpType.add, AluOpType.mult).then_inc(S["of%d%d" % (t, j)], 1)
+
+    offsets(0)
+    for t in range(NL):
+        k, h = 32 * t, 512 * t
+        if t == 0:
+            A.wait_ge(S.pgl, 128)
+        A.wait_ge(S["of%d1" % t], 1)
+        A.activation(T.hb[:, h + 256:h + 512], win.indirect(T.off[:, k + 16:k + 32]), COPY).then_inc(S["gz%d" % t], 1)
+        V.wait_ge(S["of%d0" % t], 1)
+        V.tensor_copy(T.hb[:, h:h + 256], win.indirect(T.off[:, k:k + 16])).then_inc(S["gv%d" % t], 1)
+        if 0 < t < NL - 1:
+            offsets(t + 1)
+        V.wait_ge(S["gv%d" % t], 1)
+        V.wait_ge(S["gz%d" % t], 1)
+        V.quantize_mx(T.hq[:, 128 * t:128 * t + 128], T.hp[:, 128 * t:128 * t + 128],
+                      T.hb[:, h:h + 512]).then_inc(S["hq%d" % t], 1)
+        if t == 0:
+            offsets(1)
+        d = order[t]
+        rid, pid = topo.addr(T.cores[d], core)
+        a = 128 * slot(r, d)
+        arr = S["pa%d" % slot(r, d)]
+        g.wait_ge(S["hq%d" % t], 1)
+        g.remote_dma(T.lq[:, a:a + 128].bitcast(U8), T.hq[:, 128 * t:128 * t + 128].bitcast(U8),
+                     arr, S.lpg, pid, rid, eng(d))
+        g.remote_dma(T.lp[:, a:a + 128], T.hp[:, 128 * t:128 * t + 128], arr, S.lpg, pid, rid, eng(d))
+        if t == 2:
+            one = 1 << topo.engines(core, T.cores[others[0]])[0]
+            g.wait_ge(S.dch, 16)
+            g.remote_dma_fused([RemoteDMATransfer(
+                dst_ids=[did(x) for x in order], dma_engine_mask=one, remote_sem=S.cha, srcs=[T.dd[:]],
+                dsts=[T.chd[128 * slot(r, x):128 * slot(r, x) + 128, :] for x in order])], local_sem=S.lch)
+
+    n = 32
+    Y.wait_ge(S.cea, count)
+    Y.dma_start(T.chs[0:1, 2 * efrom:2 * efrom + 2], T.ce[0:1, :]).then_inc(S.chl, 16)
+    Y.wait_ge(S.cha, NL)
+    for qs in ([q for q in range(r) if q != efrom], [q for q in range(r + 1, NR) if q != efrom]):
+        if qs:
+            lo, hi, at = slot(qs[0], r), slot(qs[-1], r), slot(r, qs[0])
+            Y.dma_start(T.chs[0:1, 2 * qs[0]:2 * qs[-1] + 2], T.chd[128 * lo + at:128 * hi + at + 1:128, :]).then_inc(S.chl, 16)
+            n += 16
+
+    P.wait_ge(S.qw, 1)
+    P.wait_ge(S.qp, 1)
+    for i in range(4):
+        j = i % 2
+        b = 512 * (1 + i)
+        if i == 2:
+            P.wait_ge(S.ea, 2 * count)
+        mq, mp = (T.pq, T.pp) if i < 2 else (T["eq"], T["ep"])
+        P.matmul_mx(T.ps[:, b:b + 512], T.wq[:, 128 * j:128 * j + 128], T.wp[:, 128 * j:128 * j + 128],
+                    mq[:], mp[:], True, True).then_inc(S["om%d" % i], 1)
+        if i != 2:
+            A.wait_ge(S["om%d" % i], 1)
+            A.activation(T.ow[:, 512 * i:512 * i + 512], T.ps[:, b:b + 512], COPY).then_inc(S["oc%d" % i], 1)
+
+    def listed(i):
+        V.wait_ge(S["oo%d" % i], 1)
+        V.wait_ge(S["oc%d" % i], 1)
+        c = 64 * (i % 2 * NR + (r if i < 2 else efrom))
+        V.tensor_copy(T.yb[:, c:c + 64], T.ow[:, 512 * i:512 * i + 512].indirect(T.offo[:, 4 * i:4 * i + 4])).then_inc(S["oy%d" % i], 1)
+        Y.wait_ge(S["oy%d" % i], 1)
+        Y.dma_start(T.y[:, c:c + 64], T.yb[:, c:c + 64]).then_inc(S.yst, 16)
+
+    V.wait_ge(S.k5, 1)
+    for i in range(4):
+        if i == 2:
+            V.wait_ge(S.cea, count)
+        src = T.bt[:, 10 + i:11 + i] if i < 2 else T.ce[:, i - 2:i - 1]
+        V.tensor_scalar(T.offo[:, 4 * i:4 * i + 4], T.if64[:], src, 64.0,
+                        AluOpType.add, AluOpType.mult).then_inc(S["oo%d" % i], 1)
+    V.wait_ge(S.om2, 1)
+    V.tensor_copy(T.ow[:, 1024:1536], T.ps[:, 1536:2048]).then_inc(S.oc2, 1)
+
+    banks = [(5, 6), (7, 0), (1, 2), (3, 4)]
+    for t in range(NL):
+        bank = banks[t]
+        q = come[t]
+        lo = 128 * slot(q, r)
+        P.wait_ge(S["pa%d" % slot(q, r)], 2 * count)
+        if t == 1:
+            P.wait_ge(S.v1, 1)
+        if t >= 2:
+            P.wait_ge(S["oc%d" % (2 * t - 4)], 1)
+            P.wait_ge(S["oc%d" % (2 * t - 3)], 1)
+        for j in range(2):
+            P.matmul_mx(T.ps[:, 512 * bank[j]:512 * bank[j] + 128], T.wq[:, 128 * j:128 * j + 128],
+                        T.wp[:, 128 * j:128 * j + 128], T.lq[:, lo:lo + 128], T.lp[:, lo:lo + 128],
+                        True, True).then_inc(S["mm%d%d" % (t, j)], 1)
+        c = 64 * q
+        b = 512 * bank[0]
+        V.wait_ge(S["mm%d0" % t], 1)
+        V.tensor_copy(T.yb[:, c:c + 64], T.ps[:, b:b + 64]).then_inc(S["cp%d0" % t], 1)
+        Y.wait_ge(S["cp%d0" % t], 1)
+        Y.dma_start(T.y[:, c:c + 64], T.yb[:, c:c + 64]).then_inc(S.yst, 16)
+        c = 64 * (NR + q)
+        b = 512 * bank[1] + 64
+        A.wait_ge(S["mm%d1" % t], 1)
+        A.activation(T.yb[:, c:c + 64], T.ps[:, b:b + 64], COPY).then_inc(S["cp%d1" % t], 1)
+        A.wait_ge(S["cp%d1" % t], 1)
+        A.dma_start(T.y[:, c:c + 64], T.yb[:, c:c + 64]).then_inc(S.yst, 16)
+        if t == 0:
+            listed(0)
+            listed(1)
+            listed(2)
+            listed(3)
+        if t == 1:
+            V.wait_ge(S.chl, n)
+            for j in range(2):
+                V.tensor_copy(T.cho[0:1, 6 * j:6 * j + 6], T.chs[0:1, j:12:2]).then_inc(S.chv, 1)
+            Y.wait_ge(S.chv, 2)
+            Y.dma_start(T.ch[:], T.cho[0:1, :]).then_inc(S.chst, 16)
+
+    g.wait_ge(S.lg, count)
+    g.wait_ge(S.le, 2 * count)
+    g.wait_ge(S.lce, count)
+    g.wait_ge(S.lpg, 2 * count * NL)
+    g.wait_ge(S.lch, 1)
+    Y.wait_ge(S.chst, 16)
+    Y.wait_ge(S.yst, 16 * 2 * NR)

@@ -2,293 +2,345 @@ from concourse.bass import DstId, RemoteDMATransfer
 from concourse.mybir import dt, AluOpType, ActivationFunctionType
 
 U8 = dt.uint8
+CODES = "float8_e4m3fn_x4"
 COPY = ActivationFunctionType.Copy
 NR = 6
-NO = NR - 1
-NL = NR - 2
+NA = 2
+NC = NR - 1 - NA
+PG, PW = 8, 64
+EARLY = 4
+SHARE = 8
 
 SCRATCH = {
     "gt": ("sbuf", [128, 512], "bfloat16"),
+    "g4": ("sbuf", [128, 552], "bfloat16"),
     "st": ("sbuf", [128, 512], "bfloat16"),
     "pgt": ("sbuf", [128, 2048], "bfloat16"),
     "wt": ("sbuf", [128, 1024], "bfloat16"),
-    "gq": ("sbuf", [128, 144], "float8_e4m3fn_x4"),
+    "gq": ("sbuf", [128, 144], CODES),
     "gp": ("sbuf", [128, 144], "uint8"),
-    "sq": ("sbuf", [128, 128], "float8_e4m3fn_x4"),
-    "sp": ("sbuf", [128, 128], "uint8"),
-    "wq": ("sbuf", [128, 256], "float8_e4m3fn_x4"),
+    "hq4": ("sbuf", [128, 138], CODES),
+    "hp4": ("sbuf", [128, 138], "uint8"),
+    "sq": ("sbuf", [128, 176], CODES),
+    "sp": ("sbuf", [128, 176], "uint8"),
+    "wq": ("sbuf", [128, 256], CODES),
     "wp": ("sbuf", [128, 256], "uint8"),
-    "pq": ("sbuf", [128, 512], "float8_e4m3fn_x4"),
+    "pq": ("sbuf", [128, 512], CODES),
     "pp": ("sbuf", [128, 512], "uint8"),
-    "eq": ("sbuf", [128, 512], "float8_e4m3fn_x4"),
-    "ep": ("sbuf", [128, 512], "uint8"),
-    "hb": ("sbuf", [128, 2048], "bfloat16"),
-    "hq": ("sbuf", [128, 512], "float8_e4m3fn_x4"),
-    "hp": ("sbuf", [128, 512], "uint8"),
-    "lq": ("sbuf", [128, 640], "float8_e4m3fn_x4"),
-    "lp": ("sbuf", [128, 640], "uint8"),
-    "ow": ("sbuf", [128, 2048], "float32"),
+    "eq": ("sbuf", [128, 1024], CODES),
+    "ep": ("sbuf", [128, 1024], "uint8"),
+    "hb": ("sbuf", [128, 1536], "bfloat16"),
+    "hq": ("sbuf", [128, 384], CODES),
+    "hp": ("sbuf", [128, 384], "uint8"),
+    "lq": ("sbuf", [128, 384], CODES),
+    "lp": ("sbuf", [128, 384], "uint8"),
+    "ow": ("sbuf", [128, 3072], "float32"),
     "yb": ("sbuf", [128, 768], "float32"),
     "sc": ("sbuf", [128, 32], "float32"),
-    "pm": ("sbuf", [128, 8], "float32"),
-    "lt": ("sbuf", [128, 64], "float32"),
-    "zz": ("sbuf", [128, 40], "float32"),
-    "bb": ("sbuf", [128, 64], "float32"),
-    "bt": ("sbuf", [128, 32], "float32"),
-    "ce": ("sbuf", [128, 2], "float32"),
+    "pm": ("sbuf", [128, 16], "float32"),
+    "lt": ("sbuf", [128, 120], "float32"),
+    "bb": ("sbuf", [128, 80], "float32"),
+    "bt": ("sbuf", [128, 64], "float32"),
     "i0": ("sbuf", [128, 16], "int32"),
     "i1": ("sbuf", [128, 16], "int32"),
     "i2": ("sbuf", [128, 16], "int32"),
     "i3": ("sbuf", [128, 16], "float32"),
     "if256": ("sbuf", [128, 16], "float32"),
     "if64": ("sbuf", [128, 4], "float32"),
-    "off": ("sbuf", [128, 128], "uint16"),
-    "offo": ("sbuf", [128, 16], "uint16"),
-    "chs": ("sbuf", [128, 12], "float32"),
-    "cho": ("sbuf", [128, 12], "float32"),
-    "chd": ("dram", [640, 2], "float32"),
-    "dd": ("dram", [128, 2], "float32"),
+    "off": ("sbuf", [128, 96], "uint16"),
+    "offo": ("sbuf", [128, 24], "uint16"),
     "ps": ("psum", [128, 4096], "float32"),
 }
-SEMAPHORES = (["gsl", "sml", "qwl", "pgl", "mg", "ms", "ml", "mz", "ii", "jj", "k2", "k3", "k4", "k5",
-               "cs", "qg", "qs", "qw", "qp", "sc", "v1", "v2", "v3", "v4", "v5",
-               "gsa", "lg", "le", "ea", "lce", "cea", "lpg", "lch", "dch", "cha", "chl", "chv", "chst", "yst"]
-              + [n + "%d" % t for n in ("gv", "gz", "hq") for t in range(NL)]
-              + ["pa%d" % t for t in range(NO)]
-              + [n + "%d%d" % (t, j) for n in ("of", "mm", "cp") for t in range(NL) for j in range(2)]
-              + [n + "%d" % t for n in ("om", "oc", "oo", "oy") for t in range(4)])
+STEPS = 100
+SEMAPHORES = (["gsl", "sml", "qwl", "pg0", "pg1", "yst", "left", "gsa", "sma", "rc", "rs"]
+              + [n + "%d" % q for n in ("e0_", "e1_") for q in range(NR)]
+              + ["pa%d" % t for t in range(NC)]
+              + ["t%d" % i for i in range(STEPS)])
+
+
+def rounds(cores, topo):
+    n = len(cores)
+    out = []
+    for k in range(n - 1):
+        pair = {}
+        for i in range(n // 2):
+            a, b = (k + i) % (n - 1), n - 1 if i == 0 else (k - i) % (n - 1)
+            pair[a], pair[b] = b, a
+        out.append(pair)
+    return sorted(out, key=lambda p: sum(topo.same_plane(cores[a], cores[b]) for a, b in p.items()))
+
+
+def helpers(core, cores, topo):
+    free = [h for h in topo.cores_of(core) if h != core and all(topo.may_write(h, d) for d in cores)]
+    return ([h for h in free if topo.die(h) != topo.die(core)][0], [h for h in free if topo.die(h) == topo.die(core)][0])
+
+
+def halves(mask):
+    e = [1 << i for i in range(mask.bit_length()) if mask >> i & 1]
+    return sum(e[:len(e) // 2]), sum(e[len(e) // 2:])
 
 
 def rank_program(g, core, T, topo):
-    r = T.rank_of(core)
-    if r is None:
-        return
     S = T.sem
-    V, A, P, Y = g.vector, g.scalar, g.tensor, g.sync
-    others = [q for q in range(NR) if q != r]
+    cores = list(T.cores)
+    home = [q for q in range(NR) if core in topo.cores_of(cores[q])]
+    if not home:
+        return
+    r = home[0]
+    far, near = helpers(cores[r], cores, topo)
+    if core not in (cores[r], far, near):
+        return
+    rs = rounds(cores, topo)
+    whole = [p[r] for p in rs[:NA]]
+    chosen = [p[r] for p in rs[NA:]]
+    others = whole + chosen
     slot = lambda q, at: q - (q > at)
-    order = [(r + 1 + t) % NR for t in range(NL)]
-    come = [(r - 1 - t) % NR for t in range(NL)]
-    eto = (r + NO) % NR
-    efrom = (r + 1) % NR
-    eng = lambda d: topo.mask(core, T.cores[d])
-    allmask = eng(others[0])
+    off_chip = topo.mask(core, cores[others[0]])
     for d in others:
-        allmask &= eng(d)
-    count = bin(allmask).count("1")
+        off_chip &= topo.mask(core, cores[d])
+    count = bin(off_chip).count("1")
+    sent = [0]
 
-    def did(d):
-        rid, pid = topo.addr(T.cores[d], core)
-        return DstId(rid=rid, pnc=pid)
+    def send(src, dsts, sem, mask):
+        ids = [DstId(rid=a[0], pnc=a[1]) for a in (topo.addr(c, core) for c, _ in dsts)]
+        g.remote_dma_fused([RemoteDMATransfer(dst_ids=ids, dma_engine_mask=mask, remote_sem=sem, srcs=[src],
+                                              dsts=[d for _, d in dsts])], local_sem=S.left)
+        sent[0] += bin(mask).count("1")
+
+    def pages_to_whole(a, b, sem, before):
+        for k, (src, dst) in enumerate(((T.pq, T["eq"]), (T.pp, T["ep"]))):
+            cast = (lambda v: v.bitcast(U8)) if k == 0 else (lambda v: v)
+            before(k)
+            send(cast(src[:, a:b]), [(cores[d], cast(dst[:, 512 * u + a:512 * u + b])) for u, d in enumerate(whole)],
+                 sem, off_chip)
+
+    cut = PW * EARLY
+    on_chip = topo.mask(cores[r], far) & ~topo.mask(cores[r], cores[others[0]])
+    lanes = bin(on_chip).count("1")
+
+    if core == far:
+        pages_to_whole(0, cut, S["e0_%d" % r], lambda k: g.wait_ge((S.rc, S.rs)[k], lanes))
+        g.wait_ge(S.left, sent[0])
+        return
+    if core == near:
+        g.wait_ge(S.rc, lanes // 2)
+        at = {d: PG * (1 + slot(r, d)) for d in others}
+        send(T.sq[:, 0:PG].bitcast(U8), [(cores[d], T.sq[:, at[d]:at[d] + PG].bitcast(U8)) for d in others], S.sma, off_chip)
+        g.wait_ge(S.rs, lanes // 2)
+        send(T.sp[:, 0:PG], [(cores[d], T.sp[:, at[d]:at[d] + PG]) for d in others], S.sma, off_chip)
+        g.wait_ge(S.left, sent[0])
+        return
+
+    V, A, P, Y = g.vector, g.scalar, g.tensor, g.sync
+    used = [0]
+
+    def done(call):
+        sem = S["t%d" % used[0]]
+        used[0] += 1
+        call.then_inc(sem, 1)
+        return sem
+
+    def after(queue, *sems):
+        for s in sems:
+            queue.wait_ge(s, 1)
+        return queue
+
+    def copy(queue, out, in_):
+        return done(V.tensor_copy(out, in_) if queue is V else A.activation(out, in_, COPY))
 
     Y.dma_start(T.gt[:, 0:8], T.gs[:, 0:8]).then_inc(S.gsl, 16)
     A.dma_start(T.st[:, 0:32], T.sm[:, 0:32]).then_inc(S.sml, 16)
-    for m in range(8):
-        (Y if m % 2 == 0 else A).dma_start(T.pgt[:, 256 * m:256 * m + 256], T.pg[128 * m:128 * m + 128, :]).then_inc(S.pgl, 16)
-    A.dma_start(T.wt[:], T.qw[:]).then_inc(S.qwl, 16)
+    for m in range(PG):
+        (Y if m % 2 == 0 else A).dma_start(T.pgt[:, 256 * m:256 * m + 256], T.pg[128 * m:128 * m + 128, :]).then_inc(
+            S.pg0 if m < EARLY else S.pg1, 16)
+    Y.dma_start(T.wt[:], T.qw[:]).then_inc(S.qwl, 16)
 
-    g.iota(T.i0[:], [[0, 16]], 0, 1).then_inc(S.ii, 1)
-    g.iota(T.i1[:], [[16, 16]], 0, 0).then_inc(S.jj, 1)
-    V.memset(T.gt[:, 8:512], 0.0).then_inc(S.mg, 1)
-    V.memset(T.st[:, 32:512], 0.0).then_inc(S.ms, 1)
-    V.memset(T.lt[:, 32:64], 0.0).then_inc(S.ml, 1)
-    V.memset(T.zz[:], 0.0).then_inc(S.mz, 1)
+    ii = done(g.iota(T.i0[:], [[0, 16]], 0, 1))
+    jj = done(g.iota(T.i1[:], [[16, 16]], 0, 0))
+    mg = done(V.memset(T.gt[:, 8:512], 0.0))
+    ms = done(V.memset(T.st[:, 32:512], 0.0))
+    m4 = done(V.memset(T.g4[:], 0.0))
+    after(V, mg).wait_ge(S.gsl, 16)
+    qg = done(V.quantize_mx(T.gq[:, 16:144], T.gp[:, 16:144], T.gt[:]))
+    lo, hi = halves(off_chip)
+    after(g, qg)
+    send(T.gq[:, 16:18].bitcast(U8),
+         [(cores[d], T.gq[:, 10 + 2 * t:12 + 2 * t].bitcast(U8)) for t, d in enumerate(chosen)], S.gsa, lo)
+    send(T.gp[:, 16:18], [(cores[d], T.gp[:, 10 + 2 * t:12 + 2 * t]) for t, d in enumerate(chosen)], S.gsa, hi)
 
-    V.wait_ge(S.mg, 1)
-    V.wait_ge(S.gsl, 16)
-    V.quantize_mx(T.gq[:, 16:144], T.gp[:, 16:144], T.gt[:]).then_inc(S.qg, 1)
-    g.wait_ge(S.qg, 1)
-    ids = [did(d) for d in others]
-    at = [6 + 2 * slot(r, d) for d in others]
-    half = [e for e in range(allmask.bit_length()) if allmask >> e & 1]
-    half = [sum(1 << e for e in half[:count // 2]), sum(1 << e for e in half[count // 2:])]
-    g.remote_dma_fused([RemoteDMATransfer(dst_ids=ids, dma_engine_mask=half[0], remote_sem=S.gsa,
-                                          srcs=[T.gq[:, 16:18].bitcast(U8)],
-                                          dsts=[T.gq[:, a:a + 2].bitcast(U8) for a in at])], local_sem=S.lg)
-    g.remote_dma_fused([RemoteDMATransfer(dst_ids=ids, dma_engine_mask=half[1], remote_sem=S.gsa,
-                                          srcs=[T.gp[:, 16:18]],
-                                          dsts=[T.gp[:, a:a + 2] for a in at])], local_sem=S.lg)
+    after(A, ms).wait_ge(S.sml, 16)
+    cs = [copy(A, T.st[:, 128 * a:128 * a + 32], T.st[:, 0:32]) for a in range(1, 4)]
+    after(A, m4).wait_ge(S.gsl, 16)
+    c4 = [copy(A, T.g4[:, 128 * a + 40:128 * a + 48], T.gt[:, 0:8]) for a in range(4)]
+    ml = done(V.memset(T["lt"][:], 0.0))
+    qs = done(after(V, *cs).quantize_mx(T.sq[:, 48:176], T.sp[:, 48:176], T.st[:]))
+    lo, hi = halves(on_chip)
+    after(g, qs)
+    send(T.sq[:, 48:56].bitcast(U8), [(near, T.sq[:, 0:PG].bitcast(U8))], S.rc, lo)
+    send(T.sp[:, 48:56], [(near, T.sp[:, 0:PG])], S.rs, hi)
 
-    V.wait_ge(S.ii, 1)
-    V.tensor_scalar(T.i2[:], T.i0[:], 15, None, AluOpType.bitwise_and).then_inc(S.k2, 1)
-    V.wait_ge(S.k2, 1)
-    V.wait_ge(S.jj, 1)
-    V.tensor_tensor(T.i3[:], T.i2[:], T.i1[:], AluOpType.add).then_inc(S.k3, 1)
-    V.wait_ge(S.k3, 1)
-    V.tensor_scalar(T.if256[:], T.i3[:], 1.0 / 256, None, AluOpType.mult).then_inc(S.k4, 1)
-    V.tensor_scalar(T.if64[:], T.i3[:, 0:4], 1.0 / 64, None, AluOpType.mult).then_inc(S.k5, 1)
+    k2 = done(after(V, ii).tensor_scalar(T.i2[:], T.i0[:], 15, None, AluOpType.bitwise_and))
+    k3 = done(after(V, k2, jj).tensor_tensor(T.i3[:], T.i2[:], T.i1[:], AluOpType.add))
+    k4 = done(after(V, k3).tensor_scalar(T.if256[:], T.i3[:], 1.0 / 256, None, AluOpType.mult))
+    k5 = done(V.tensor_scalar(T.if64[:], T.i3[:, 0:4], 1.0 / 64, None, AluOpType.mult))
 
-    V.wait_ge(S.ms, 1)
-    V.wait_ge(S.sml, 16)
-    for a in range(1, 4):
-        V.tensor_copy(T.st[:, 128 * a:128 * a + 32], T.st[:, 0:32]).then_inc(S.cs, 1)
-    V.wait_ge(S.cs, 3)
-    V.quantize_mx(T.sq[:], T.sp[:], T.st[:]).then_inc(S.qs, 1)
-    V.wait_ge(S.pgl, 128)
-    V.quantize_mx(T.pq[:], T.pp[:], T.pgt[:]).then_inc(S.qp, 1)
+    V.wait_ge(S.pg0, 16 * EARLY)
+    qp0 = done(V.quantize_mx(T.pq[:, 0:cut], T.pp[:, 0:cut], T.pgt[:, 0:4 * cut]))
+    q4 = done(after(V, *c4).quantize_mx(T.hq4[:], T.hp4[:], T.g4[:]))
+    V.wait_ge(S.pg1, 16 * (PG - EARLY))
+    qp1 = done(V.quantize_mx(T.pq[:, cut:512], T.pp[:, cut:512], T.pgt[:, 4 * cut:2048]))
     V.wait_ge(S.qwl, 16)
-    V.quantize_mx(T.wq[:], T.wp[:], T.wt[:]).then_inc(S.qw, 1)
+    qw = done(V.quantize_mx(T.wq[:], T.wp[:], T.wt[:]))
+    after(g, qp0)
+    send(T.pq[:, 0:cut].bitcast(U8), [(far, T.pq[:, 0:cut].bitcast(U8))], S.rc, on_chip)
+    send(T.pp[:, 0:cut], [(far, T.pp[:, 0:cut])], S.rs, on_chip)
+    after(g, qp1)
+    pages_to_whole(cut, 512, S["e1_%d" % r], lambda k: None)
 
-    rid, pid = topo.addr(T.cores[eto], core)
-    g.wait_ge(S.qp, 1)
-    g.remote_dma(T["eq"][:].bitcast(U8), T.pq[:].bitcast(U8), S.ea, S.le, pid, rid, eng(eto))
-    g.remote_dma(T["ep"][:], T.pp[:], S.ea, S.le, pid, rid, eng(eto))
+    readers = []
 
-    P.wait_ge(S.qs, 1)
-    P.wait_ge(S.qg, 1)
-    P.wait_ge(S.gsa, count * NO)
-    P.matmul_mx(T.ps[:, 0:138], T.sq[:], T.sp[:], T.gq[:, 6:144], T.gp[:, 6:144], True, True).then_inc(S.sc, 1)
+    def bank():
+        b = len(readers)
+        if b >= 8:
+            after(P, readers[b - 8][0])
+        readers.append([])
+        return 512 * (b % 8), readers[-1]
 
-    V.wait_ge(S.sc, 1)
-    V.transpose(T["sc"][:], T.ps[:, 0:32]).then_inc(S.v1, 1)
-    V.wait_ge(S.v1, 1)
-    V.tensor_tensor_scan(T["pm"][:], T["sc"][:, 0:8], T["sc"][:, 0:8], T["sc"][:, 0:1],
-                         AluOpType.max, AluOpType.max).then_inc(S.v2, 1)
-    V.wait_ge(S.v2, 1)
-    V.tensor_scalar(T["lt"][:, 24:32], T["pm"][:], T["pm"][:, 7:8], None, AluOpType.is_lt).then_inc(S.v3, 1)
-    V.wait_ge(S.ml, 1)
-    V.wait_ge(S.mz, 1)
-    V.wait_ge(S.v3, 1)
-    V.tensor_tensor_scan(T.bb[:, 24:64], T["lt"][:, 24:64], T.zz[:], 0.0,
-                         AluOpType.add, AluOpType.add).then_inc(S.v4, 1)
-    V.wait_ge(S.v4, 1)
-    V.transpose(T.bt[:], T.bb[:, 32:64]).then_inc(S.v5, 1)
+    def times_queries(j, mq, mp, a, b):
+        at, rd = bank()
+        return at, rd, done(P.matmul_mx(T.ps[:, at:at + b - a], T.wq[:, 128 * j:128 * j + 128], T.wp[:, 128 * j:128 * j + 128],
+                                        mq[:, a:b], mp[:, a:b], True, True))
 
-    Y.wait_ge(S.v5, 1)
-    Y.dma_start(T.dd[:], T.bt[0:8, 0:32]).then_inc(S.dch, 16)
-    Y.dma_start(T.chs[0:1, 2 * r:2 * r + 2], T.bt[0:1, 10:12]).then_inc(S.chl, 16)
-    g.wait_ge(S.v5, 1)
-    c = 2 * slot(eto, r)
-    g.remote_dma(T.ce[:], T.bt[:, c:c + 2], S.cea, S.lce, pid, rid, eng(eto))
+    def take(queue, out, product, a, b):
+        at, rd, mm = product
+        rd.append(copy(after(queue, mm), out, T.ps[:, at + a:at + b]))
+        return rd[0]
 
-    V.wait_ge(S.k4, 1)
-    V.wait_ge(S.v5, 1)
+    def lowest_best(k, scores, first, ready):
+        pm, lt, bb, zz = T["pm"][:, 8 * k:8 * k + 8], T["lt"], T.bb, T["lt"][:, 80:120]
+        v2 = done(after(V, ready).tensor_tensor_scan(pm, lt[:, 80:88], scores, first, AluOpType.add, AluOpType.max))
+        v3 = done(after(V, v2).tensor_scalar(lt[:, 40 * k:40 * k + 8], pm, T["pm"][:, 8 * k + 7:8 * k + 8], None, AluOpType.is_lt))
+        v4 = done(after(V, v3).tensor_tensor_scan(bb[:, 40 * k:40 * k + 40], lt[:, 40 * k:40 * k + 40], zz, 0.0,
+                                                  AluOpType.add, AluOpType.add))
+        v5 = done(after(V, v4).transpose(T.bt[:, 32 * k:32 * k + 32], bb[:, 40 * k + 8:40 * k + 40]))
+        return v2, v4, v5
+
+    after(P, qw, qp0, qp1)
+    ready = {}
+    for j in range(2):
+        ready[r, j] = [take(A, T.ow[:, 512 * j:512 * j + 512], times_queries(j, T.pq, T.pp, 0, 512), 0, 512)]
+
+    at, rd = bank()
+    after(P, qs, qg).wait_ge(S.gsa, count * NC)
+    mm = done(P.matmul_mx(T.ps[:, at:at + 128], T.sq[:, 48:176], T.sp[:, 48:176], T.gq[:, 10:138], T.gp[:, 10:138], True, True))
+    rd.append(done(after(V, mm).transpose(T["sc"][:], T.ps[:, at:at + 32])))
+    after(V, ml)
+    _, _, chose = lowest_best(0, T["sc"][:, 0:8], T["sc"][:, 0:1], rd[0])
+
     win = T.pgt[:, 0:2048]
 
-    def offsets(t):
-        for j in (1, 0):
-            c = 2 * slot(order[t], r) + j
-            k = 32 * t + 16 * j
-            V.tensor_scalar(T.off[:, k:k + 16], T.if256[:], T.bt[:, c:c + 1], 256.0,
-                            AluOpType.add, AluOpType.mult).then_inc(S["of%d%d" % (t, j)], 1)
+    def offsets(i):
+        return done(V.tensor_scalar(T.off[:, 16 * i:16 * i + 16], T.if256[:], T.bt[:, i:i + 1], 256.0,
+                                    AluOpType.add, AluOpType.mult))
 
-    offsets(0)
-    for t in range(NL):
-        k, h = 32 * t, 512 * t
+    def gather(queue, i, a, b):
+        return copy(after(queue, off[i]), T.hb[:, 256 * i + 16 * a:256 * i + 16 * b],
+                    win.indirect(T.off[:, 16 * i + a:16 * i + b]))
+
+    after(V, k4, chose)
+    off = {i: offsets(i) for i in (1, 0, 3)}
+    A.wait_ge(S.pg0, 16 * EARLY)
+    A.wait_ge(S.pg1, 16 * (PG - EARLY))
+    for t, d in enumerate(chosen):
+        last = t == NC - 1
+        got = [gather(A, 2 * t + 1, 0, 16)]
+        if last and SHARE < 16:
+            got.append(gather(A, 2 * t, SHARE, 16))
+        got.append(gather(V, 2 * t, 0, SHARE if last else 16))
         if t == 0:
-            A.wait_ge(S.pgl, 128)
-        A.wait_ge(S["of%d1" % t], 1)
-        A.activation(T.hb[:, h + 256:h + 512], win.indirect(T.off[:, k + 16:k + 32]), COPY).then_inc(S["gz%d" % t], 1)
-        V.wait_ge(S["of%d0" % t], 1)
-        V.tensor_copy(T.hb[:, h:h + 256], win.indirect(T.off[:, k:k + 16])).then_inc(S["gv%d" % t], 1)
-        if 0 < t < NL - 1:
-            offsets(t + 1)
-        V.wait_ge(S["gv%d" % t], 1)
-        V.wait_ge(S["gz%d" % t], 1)
-        V.quantize_mx(T.hq[:, 128 * t:128 * t + 128], T.hp[:, 128 * t:128 * t + 128],
-                      T.hb[:, h:h + 512]).then_inc(S["hq%d" % t], 1)
-        if t == 0:
-            offsets(1)
-        d = order[t]
-        rid, pid = topo.addr(T.cores[d], core)
-        a = 128 * slot(r, d)
-        arr = S["pa%d" % slot(r, d)]
-        g.wait_ge(S["hq%d" % t], 1)
-        g.remote_dma(T.lq[:, a:a + 128].bitcast(U8), T.hq[:, 128 * t:128 * t + 128].bitcast(U8),
-                     arr, S.lpg, pid, rid, eng(d))
-        g.remote_dma(T.lp[:, a:a + 128], T.hp[:, 128 * t:128 * t + 128], arr, S.lpg, pid, rid, eng(d))
-        if t == 2:
-            one = 1 << topo.engines(core, T.cores[others[0]])[0]
-            g.wait_ge(S.dch, 16)
-            g.remote_dma_fused([RemoteDMATransfer(
-                dst_ids=[did(x) for x in order], dma_engine_mask=one, remote_sem=S.cha, srcs=[T.dd[:]],
-                dsts=[T.chd[128 * slot(r, x):128 * slot(r, x) + 128, :] for x in order])], local_sem=S.lch)
+            off.update({i: offsets(i) for i in (2, 5, 4)})
+        hq = done(after(V, *got).quantize_mx(T.hq[:, 128 * t:128 * t + 128], T.hp[:, 128 * t:128 * t + 128],
+                                             T.hb[:, 512 * t:512 * t + 512]))
+        after(g, hq)
+        send(T.hq[:, 128 * t:128 * t + 128].bitcast(U8), [(cores[d], T.lq[:, 128 * t:128 * t + 128].bitcast(U8))],
+             S["pa%d" % t], off_chip)
+        send(T.hp[:, 128 * t:128 * t + 128], [(cores[d], T.lp[:, 128 * t:128 * t + 128])], S["pa%d" % t], off_chip)
 
-    n = 32
-    Y.wait_ge(S.cea, count)
-    Y.dma_start(T.chs[0:1, 2 * efrom:2 * efrom + 2], T.ce[0:1, :]).then_inc(S.chl, 16)
-    Y.wait_ge(S.cha, NL)
-    for qs in ([q for q in range(r) if q != efrom], [q for q in range(r + 1, NR) if q != efrom]):
-        if qs:
-            lo, hi, at = slot(qs[0], r), slot(qs[-1], r), slot(r, qs[0])
-            Y.dma_start(T.chs[0:1, 2 * qs[0]:2 * qs[-1] + 2], T.chd[128 * lo + at:128 * hi + at + 1:128, :]).then_inc(S.chl, 16)
-            n += 16
+    stores = [0]
 
-    P.wait_ge(S.qw, 1)
-    P.wait_ge(S.qp, 1)
-    for i in range(4):
-        j = i % 2
-        b = 512 * (1 + i)
-        if i == 2:
-            P.wait_ge(S.ea, 2 * count)
-        mq, mp = (T.pq, T.pp) if i < 2 else (T["eq"], T["ep"])
-        P.matmul_mx(T.ps[:, b:b + 512], T.wq[:, 128 * j:128 * j + 128], T.wp[:, 128 * j:128 * j + 128],
-                    mq[:], mp[:], True, True).then_inc(S["om%d" % i], 1)
-        if i != 2:
-            A.wait_ge(S["om%d" % i], 1)
-            A.activation(T.ow[:, 512 * i:512 * i + 512], T.ps[:, b:b + 512], COPY).then_inc(S["oc%d" % i], 1)
+    def store(queue, q, j, sem):
+        c = PW * (j * NR + q)
+        after(queue, sem).dma_start(T.y[:, c:c + PW], T.yb[:, c:c + PW]).then_inc(S.yst, 16)
+        stores[0] += 16
 
-    def listed(i):
-        V.wait_ge(S["oo%d" % i], 1)
-        V.wait_ge(S["oc%d" % i], 1)
-        c = 64 * (i % 2 * NR + (r if i < 2 else efrom))
-        V.tensor_copy(T.yb[:, c:c + 64], T.ow[:, 512 * i:512 * i + 512].indirect(T.offo[:, 4 * i:4 * i + 4])).then_inc(S["oy%d" % i], 1)
-        Y.wait_ge(S["oy%d" % i], 1)
-        Y.dma_start(T.y[:, c:c + 64], T.yb[:, c:c + 64]).then_inc(S.yst, 16)
+    listed = {}
 
-    V.wait_ge(S.k5, 1)
-    for i in range(4):
-        if i == 2:
-            V.wait_ge(S.cea, count)
-        src = T.bt[:, 10 + i:11 + i] if i < 2 else T.ce[:, i - 2:i - 1]
-        V.tensor_scalar(T.offo[:, 4 * i:4 * i + 4], T.if64[:], src, 64.0,
-                        AluOpType.add, AluOpType.mult).then_inc(S["oo%d" % i], 1)
-    V.wait_ge(S.om2, 1)
-    V.tensor_copy(T.ow[:, 1024:1536], T.ps[:, 1536:2048]).then_inc(S.oc2, 1)
+    def list_of(q, j, column):
+        i = len(listed)
+        listed[q, j] = (i, done(V.tensor_scalar(T.offo[:, 4 * i:4 * i + 4], T.if64[:], T.bt[:, column:column + 1], 64.0,
+                                                AluOpType.add, AluOpType.mult)))
 
-    banks = [(5, 6), (7, 0), (1, 2), (3, 4)]
-    for t in range(NL):
-        bank = banks[t]
-        q = come[t]
-        lo = 128 * slot(q, r)
-        P.wait_ge(S["pa%d" % slot(q, r)], 2 * count)
-        if t == 1:
-            P.wait_ge(S.v1, 1)
-        if t >= 2:
-            P.wait_ge(S["oc%d" % (2 * t - 4)], 1)
-            P.wait_ge(S["oc%d" % (2 * t - 3)], 1)
+    def pick(queue, q, j):
+        i, sem = listed[q, j]
+        w = 1024 * (0 if q == r else 1 + whole.index(q)) + 512 * j
+        c = PW * (j * NR + q)
+        after(queue, sem, *ready[q, j])
+        store(Y, q, j, copy(queue, T.yb[:, c:c + PW], T.ow[:, w:w + 512].indirect(T.offo[:, 4 * i:4 * i + 4])))
+
+    def own_picks():
+        after(V, k5)
         for j in range(2):
-            P.matmul_mx(T.ps[:, 512 * bank[j]:512 * bank[j] + 128], T.wq[:, 128 * j:128 * j + 128],
-                        T.wp[:, 128 * j:128 * j + 128], T.lq[:, lo:lo + 128], T.lp[:, lo:lo + 128],
-                        True, True).then_inc(S["mm%d%d" % (t, j)], 1)
-        c = 64 * q
-        b = 512 * bank[0]
-        V.wait_ge(S["mm%d0" % t], 1)
-        V.tensor_copy(T.yb[:, c:c + 64], T.ps[:, b:b + 64]).then_inc(S["cp%d0" % t], 1)
-        Y.wait_ge(S["cp%d0" % t], 1)
-        Y.dma_start(T.y[:, c:c + 64], T.yb[:, c:c + 64]).then_inc(S.yst, 16)
-        c = 64 * (NR + q)
-        b = 512 * bank[1] + 64
-        A.wait_ge(S["mm%d1" % t], 1)
-        A.activation(T.yb[:, c:c + 64], T.ps[:, b:b + 64], COPY).then_inc(S["cp%d1" % t], 1)
-        A.wait_ge(S["cp%d1" % t], 1)
-        A.dma_start(T.y[:, c:c + 64], T.yb[:, c:c + 64]).then_inc(S.yst, 16)
-        if t == 0:
-            listed(0)
-            listed(1)
-            listed(2)
-            listed(3)
-        if t == 1:
-            V.wait_ge(S.chl, n)
-            for j in range(2):
-                V.tensor_copy(T.cho[0:1, 6 * j:6 * j + 6], T.chs[0:1, j:12:2]).then_inc(S.chv, 1)
-            Y.wait_ge(S.chv, 2)
-            Y.dma_start(T.ch[:], T.cho[0:1, :]).then_inc(S.chst, 16)
+            list_of(r, j, 2 * NC + j)
+        for j in range(2):
+            pick(A, r, j)
 
-    g.wait_ge(S.lg, count)
-    g.wait_ge(S.le, 2 * count)
-    g.wait_ge(S.lce, count)
-    g.wait_ge(S.lpg, 2 * count * NL)
-    g.wait_ge(S.lch, 1)
-    Y.wait_ge(S.chst, 16)
-    Y.wait_ge(S.yst, 16 * 2 * NR)
+    def choices():
+        at, rd = bank()
+        after(P, q4).wait_ge(S.sma, 2 * count * (NR - 1))
+        for q in range(NR):
+            s = PG * (NR if q == r else 1 + slot(q, r))
+            mm = P.matmul_mx(T.ps[:, at:at + 128], T.hq4[:, 10 - 2 * q:138 - 2 * q], T.hp4[:, 10 - 2 * q:138 - 2 * q],
+                             T.sq[:, s:s + 128], T.sp[:, s:s + 128], q == 0, q == NR - 1)
+        v2, v4, v5 = lowest_best(1, T.ps[:, at:at + 8], T.ps[:, at:at + 1], done(mm))
+        rd.append(v2)
+        after(Y, v4)
+        for j in range(2):
+            Y.dma_start(T.ch[j:j + 1, :], T.bb[j:2 * NR:2, 79:80]).then_inc(S.yst, 16)
+            stores[0] += 16
+        after(V, v5)
+        for q in whole:
+            for j in range(2):
+                list_of(q, j, 32 + 2 * q + j)
+
+    def part(name, a, b, queues):
+        for u, q in enumerate(whole):
+            P.wait_ge(S[name % q], 2 * count)
+            for j in range(2):
+                w = 1024 * (1 + u) + 512 * j
+                product = times_queries(j, T["eq"], T["ep"], 512 * u + a, 512 * u + b)
+                ready.setdefault((q, j), []).append(take(queues[2 * u + j], T.ow[:, w + a:w + b], product, 0, b - a))
+
+    def picks():
+        for q in whole:
+            pick(V, q, 0)
+            pick(A, q, 1)
+
+    def arrived(t):
+        P.wait_ge(S["pa%d" % t], 2 * count)
+        q = chosen[t]
+        for j, queue in enumerate((V, A)):
+            c = PW * (j * NR + q)
+            sem = take(queue, T.yb[:, c:c + PW], times_queries(j, T.lq, T.lp, 128 * t, 128 * t + 128), PW * j, PW * j + PW)
+            store(A if (t, j) == (NC - 1, 1) else Y, q, j, sem)
+
+    own_picks()
+    part("e1_%d", cut, 512, (A, A, V, A))
+    choices()
+    arrived(0)
+    part("e0_%d", 0, cut, (V, A, V, A))
+    picks()
+    arrived(1)
+    arrived(2)
+
+    g.wait_ge(S.left, sent[0])
+    Y.wait_ge(S.yst, stores[0])

from concourse.bass import DstId, RemoteDMATransfer
from concourse.mybir import dt, AluOpType, ActivationFunctionType

U8 = dt.uint8
CODES = "float8_e4m3fn_x4"
COPY = ActivationFunctionType.Copy
NR = 6
NA = 2
NC = NR - 1 - NA
PG, PW = 8, 64
EARLY = 4
SHARE = 8

SCRATCH = {
    "gt": ("sbuf", [128, 512], "bfloat16"),
    "g4": ("sbuf", [128, 552], "bfloat16"),
    "st": ("sbuf", [128, 512], "bfloat16"),
    "pgt": ("sbuf", [128, 2048], "bfloat16"),
    "wt": ("sbuf", [128, 1024], "bfloat16"),
    "gq": ("sbuf", [128, 144], CODES),
    "gp": ("sbuf", [128, 144], "uint8"),
    "hq4": ("sbuf", [128, 138], CODES),
    "hp4": ("sbuf", [128, 138], "uint8"),
    "sq": ("sbuf", [128, 176], CODES),
    "sp": ("sbuf", [128, 176], "uint8"),
    "wq": ("sbuf", [128, 256], CODES),
    "wp": ("sbuf", [128, 256], "uint8"),
    "pq": ("sbuf", [128, 512], CODES),
    "pp": ("sbuf", [128, 512], "uint8"),
    "eq": ("sbuf", [128, 1024], CODES),
    "ep": ("sbuf", [128, 1024], "uint8"),
    "hb": ("sbuf", [128, 1536], "bfloat16"),
    "hq": ("sbuf", [128, 384], CODES),
    "hp": ("sbuf", [128, 384], "uint8"),
    "lq": ("sbuf", [128, 384], CODES),
    "lp": ("sbuf", [128, 384], "uint8"),
    "ow": ("sbuf", [128, 3072], "float32"),
    "yb": ("sbuf", [128, 768], "float32"),
    "sc": ("sbuf", [128, 32], "float32"),
    "pm": ("sbuf", [128, 16], "float32"),
    "lt": ("sbuf", [128, 120], "float32"),
    "bb": ("sbuf", [128, 80], "float32"),
    "bt": ("sbuf", [128, 64], "float32"),
    "i0": ("sbuf", [128, 16], "int32"),
    "i1": ("sbuf", [128, 16], "int32"),
    "i2": ("sbuf", [128, 16], "int32"),
    "i3": ("sbuf", [128, 16], "float32"),
    "if256": ("sbuf", [128, 16], "float32"),
    "if64": ("sbuf", [128, 4], "float32"),
    "off": ("sbuf", [128, 96], "uint16"),
    "offo": ("sbuf", [128, 24], "uint16"),
    "ps": ("psum", [128, 4096], "float32"),
}
STEPS = 100
SEMAPHORES = (["gsl", "sml", "qwl", "pg0", "pg1", "yst", "left", "gsa", "sma", "rc", "rs"]
              + [n + "%d" % q for n in ("e0_", "e1_") for q in range(NR)]
              + ["pa%d" % t for t in range(NC)]
              + ["t%d" % i for i in range(STEPS)])


def rounds(cores, topo):
    n = len(cores)
    out = []
    for k in range(n - 1):
        pair = {}
        for i in range(n // 2):
            a, b = (k + i) % (n - 1), n - 1 if i == 0 else (k - i) % (n - 1)
            pair[a], pair[b] = b, a
        out.append(pair)
    return sorted(out, key=lambda p: sum(topo.same_plane(cores[a], cores[b]) for a, b in p.items()))


def helpers(core, cores, topo):
    free = [h for h in topo.cores_of(core) if h != core and all(topo.may_write(h, d) for d in cores)]
    return ([h for h in free if topo.die(h) != topo.die(core)][0], [h for h in free if topo.die(h) == topo.die(core)][0])


def halves(mask):
    e = [1 << i for i in range(mask.bit_length()) if mask >> i & 1]
    return sum(e[:len(e) // 2]), sum(e[len(e) // 2:])


def rank_program(g, core, T, topo):
    S = T.sem
    cores = list(T.cores)
    home = [q for q in range(NR) if core in topo.cores_of(cores[q])]
    if not home:
        return
    r = home[0]
    far, near = helpers(cores[r], cores, topo)
    if core not in (cores[r], far, near):
        return
    rs = rounds(cores, topo)
    whole = [p[r] for p in rs[:NA]]
    chosen = [p[r] for p in rs[NA:]]
    others = whole + chosen
    slot = lambda q, at: q - (q > at)
    off_chip = topo.mask(core, cores[others[0]])
    for d in others:
        off_chip &= topo.mask(core, cores[d])
    count = bin(off_chip).count("1")
    sent = [0]

    def send(src, dsts, sem, mask):
        ids = [DstId(rid=a[0], pnc=a[1]) for a in (topo.addr(c, core) for c, _ in dsts)]
        g.remote_dma_fused([RemoteDMATransfer(dst_ids=ids, dma_engine_mask=mask, remote_sem=sem, srcs=[src],
                                              dsts=[d for _, d in dsts])], local_sem=S.left)
        sent[0] += bin(mask).count("1")

    def pages_to_whole(a, b, sem, before):
        for k, (src, dst) in enumerate(((T.pq, T["eq"]), (T.pp, T["ep"]))):
            cast = (lambda v: v.bitcast(U8)) if k == 0 else (lambda v: v)
            before(k)
            send(cast(src[:, a:b]), [(cores[d], cast(dst[:, 512 * u + a:512 * u + b])) for u, d in enumerate(whole)],
                 sem, off_chip)

    cut = PW * EARLY
    on_chip = topo.mask(cores[r], far) & ~topo.mask(cores[r], cores[others[0]])
    lanes = bin(on_chip).count("1")

    if core == far:
        pages_to_whole(0, cut, S["e0_%d" % r], lambda k: g.wait_ge((S.rc, S.rs)[k], lanes))
        g.wait_ge(S.left, sent[0])
        return
    if core == near:
        g.wait_ge(S.rc, lanes // 2)
        at = {d: PG * (1 + slot(r, d)) for d in others}
        send(T.sq[:, 0:PG].bitcast(U8), [(cores[d], T.sq[:, at[d]:at[d] + PG].bitcast(U8)) for d in others], S.sma, off_chip)
        g.wait_ge(S.rs, lanes // 2)
        send(T.sp[:, 0:PG], [(cores[d], T.sp[:, at[d]:at[d] + PG]) for d in others], S.sma, off_chip)
        g.wait_ge(S.left, sent[0])
        return

    V, A, P, Y = g.vector, g.scalar, g.tensor, g.sync
    used = [0]

    def done(call):
        sem = S["t%d" % used[0]]
        used[0] += 1
        call.then_inc(sem, 1)
        return sem

    def after(queue, *sems):
        for s in sems:
            queue.wait_ge(s, 1)
        return queue

    def copy(queue, out, in_):
        return done(V.tensor_copy(out, in_) if queue is V else A.activation(out, in_, COPY))

    Y.dma_start(T.gt[:, 0:8], T.gs[:, 0:8]).then_inc(S.gsl, 16)
    A.dma_start(T.st[:, 0:32], T.sm[:, 0:32]).then_inc(S.sml, 16)
    for m in range(PG):
        (Y if m % 2 == 0 else A).dma_start(T.pgt[:, 256 * m:256 * m + 256], T.pg[128 * m:128 * m + 128, :]).then_inc(
            S.pg0 if m < EARLY else S.pg1, 16)
    Y.dma_start(T.wt[:], T.qw[:]).then_inc(S.qwl, 16)

    ii = done(g.iota(T.i0[:], [[0, 16]], 0, 1))
    jj = done(g.iota(T.i1[:], [[16, 16]], 0, 0))
    mg = done(V.memset(T.gt[:, 8:512], 0.0))
    ms = done(V.memset(T.st[:, 32:512], 0.0))
    m4 = done(V.memset(T.g4[:], 0.0))
    after(V, mg).wait_ge(S.gsl, 16)
    qg = done(V.quantize_mx(T.gq[:, 16:144], T.gp[:, 16:144], T.gt[:]))
    lo, hi = halves(off_chip)
    after(g, qg)
    send(T.gq[:, 16:18].bitcast(U8),
         [(cores[d], T.gq[:, 10 + 2 * t:12 + 2 * t].bitcast(U8)) for t, d in enumerate(chosen)], S.gsa, lo)
    send(T.gp[:, 16:18], [(cores[d], T.gp[:, 10 + 2 * t:12 + 2 * t]) for t, d in enumerate(chosen)], S.gsa, hi)

    after(A, ms).wait_ge(S.sml, 16)
    cs = [copy(A, T.st[:, 128 * a:128 * a + 32], T.st[:, 0:32]) for a in range(1, 4)]
    after(A, m4).wait_ge(S.gsl, 16)
    c4 = [copy(A, T.g4[:, 128 * a + 40:128 * a + 48], T.gt[:, 0:8]) for a in range(4)]
    ml = done(V.memset(T["lt"][:], 0.0))
    qs = done(after(V, *cs).quantize_mx(T.sq[:, 48:176], T.sp[:, 48:176], T.st[:]))
    lo, hi = halves(on_chip)
    after(g, qs)
    send(T.sq[:, 48:56].bitcast(U8), [(near, T.sq[:, 0:PG].bitcast(U8))], S.rc, lo)
    send(T.sp[:, 48:56], [(near, T.sp[:, 0:PG])], S.rs, hi)

    k2 = done(after(V, ii).tensor_scalar(T.i2[:], T.i0[:], 15, None, AluOpType.bitwise_and))
    k3 = done(after(V, k2, jj).tensor_tensor(T.i3[:], T.i2[:], T.i1[:], AluOpType.add))
    k4 = done(after(V, k3).tensor_scalar(T.if256[:], T.i3[:], 1.0 / 256, None, AluOpType.mult))
    k5 = done(V.tensor_scalar(T.if64[:], T.i3[:, 0:4], 1.0 / 64, None, AluOpType.mult))

    V.wait_ge(S.pg0, 16 * EARLY)
    qp0 = done(V.quantize_mx(T.pq[:, 0:cut], T.pp[:, 0:cut], T.pgt[:, 0:4 * cut]))
    q4 = done(after(V, *c4).quantize_mx(T.hq4[:], T.hp4[:], T.g4[:]))
    V.wait_ge(S.pg1, 16 * (PG - EARLY))
    qp1 = done(V.quantize_mx(T.pq[:, cut:512], T.pp[:, cut:512], T.pgt[:, 4 * cut:2048]))
    V.wait_ge(S.qwl, 16)
    qw = done(V.quantize_mx(T.wq[:], T.wp[:], T.wt[:]))
    after(g, qp0)
    send(T.pq[:, 0:cut].bitcast(U8), [(far, T.pq[:, 0:cut].bitcast(U8))], S.rc, on_chip)
    send(T.pp[:, 0:cut], [(far, T.pp[:, 0:cut])], S.rs, on_chip)
    after(g, qp1)
    pages_to_whole(cut, 512, S["e1_%d" % r], lambda k: None)

    readers = []

    def bank():
        b = len(readers)
        if b >= 8:
            after(P, readers[b - 8][0])
        readers.append([])
        return 512 * (b % 8), readers[-1]

    def times_queries(j, mq, mp, a, b):
        at, rd = bank()
        return at, rd, done(P.matmul_mx(T.ps[:, at:at + b - a], T.wq[:, 128 * j:128 * j + 128], T.wp[:, 128 * j:128 * j + 128],
                                        mq[:, a:b], mp[:, a:b], True, True))

    def take(queue, out, product, a, b):
        at, rd, mm = product
        rd.append(copy(after(queue, mm), out, T.ps[:, at + a:at + b]))
        return rd[0]

    def lowest_best(k, scores, first, ready):
        pm, lt, bb, zz = T["pm"][:, 8 * k:8 * k + 8], T["lt"], T.bb, T["lt"][:, 80:120]
        v2 = done(after(V, ready).tensor_tensor_scan(pm, lt[:, 80:88], scores, first, AluOpType.add, AluOpType.max))
        v3 = done(after(V, v2).tensor_scalar(lt[:, 40 * k:40 * k + 8], pm, T["pm"][:, 8 * k + 7:8 * k + 8], None, AluOpType.is_lt))
        v4 = done(after(V, v3).tensor_tensor_scan(bb[:, 40 * k:40 * k + 40], lt[:, 40 * k:40 * k + 40], zz, 0.0,
                                                  AluOpType.add, AluOpType.add))
        v5 = done(after(V, v4).transpose(T.bt[:, 32 * k:32 * k + 32], bb[:, 40 * k + 8:40 * k + 40]))
        return v2, v4, v5

    after(P, qw, qp0, qp1)
    ready = {}
    for j in range(2):
        ready[r, j] = [take(A, T.ow[:, 512 * j:512 * j + 512], times_queries(j, T.pq, T.pp, 0, 512), 0, 512)]

    at, rd = bank()
    after(P, qs, qg).wait_ge(S.gsa, count * NC)
    mm = done(P.matmul_mx(T.ps[:, at:at + 128], T.sq[:, 48:176], T.sp[:, 48:176], T.gq[:, 10:138], T.gp[:, 10:138], True, True))
    rd.append(done(after(V, mm).transpose(T["sc"][:], T.ps[:, at:at + 32])))
    after(V, ml)
    _, _, chose = lowest_best(0, T["sc"][:, 0:8], T["sc"][:, 0:1], rd[0])

    win = T.pgt[:, 0:2048]

    def offsets(i):
        return done(V.tensor_scalar(T.off[:, 16 * i:16 * i + 16], T.if256[:], T.bt[:, i:i + 1], 256.0,
                                    AluOpType.add, AluOpType.mult))

    def gather(queue, i, a, b):
        return copy(after(queue, off[i]), T.hb[:, 256 * i + 16 * a:256 * i + 16 * b],
                    win.indirect(T.off[:, 16 * i + a:16 * i + b]))

    after(V, k4, chose)
    off = {i: offsets(i) for i in (1, 0, 3)}
    A.wait_ge(S.pg0, 16 * EARLY)
    A.wait_ge(S.pg1, 16 * (PG - EARLY))
    for t, d in enumerate(chosen):
        last = t == NC - 1
        got = [gather(A, 2 * t + 1, 0, 16)]
        if last and SHARE < 16:
            got.append(gather(A, 2 * t, SHARE, 16))
        got.append(gather(V, 2 * t, 0, SHARE if last else 16))
        if t == 0:
            off.update({i: offsets(i) for i in (2, 5, 4)})
        hq = done(after(V, *got).quantize_mx(T.hq[:, 128 * t:128 * t + 128], T.hp[:, 128 * t:128 * t + 128],
                                             T.hb[:, 512 * t:512 * t + 512]))
        after(g, hq)
        send(T.hq[:, 128 * t:128 * t + 128].bitcast(U8), [(cores[d], T.lq[:, 128 * t:128 * t + 128].bitcast(U8))],
             S["pa%d" % t], off_chip)
        send(T.hp[:, 128 * t:128 * t + 128], [(cores[d], T.lp[:, 128 * t:128 * t + 128])], S["pa%d" % t], off_chip)

    stores = [0]

    def store(queue, q, j, sem):
        c = PW * (j * NR + q)
        after(queue, sem).dma_start(T.y[:, c:c + PW], T.yb[:, c:c + PW]).then_inc(S.yst, 16)
        stores[0] += 16

    listed = {}

    def list_of(q, j, column):
        i = len(listed)
        listed[q, j] = (i, done(V.tensor_scalar(T.offo[:, 4 * i:4 * i + 4], T.if64[:], T.bt[:, column:column + 1], 64.0,
                                                AluOpType.add, AluOpType.mult)))

    def pick(queue, q, j):
        i, sem = listed[q, j]
        w = 1024 * (0 if q == r else 1 + whole.index(q)) + 512 * j
        c = PW * (j * NR + q)
        after(queue, sem, *ready[q, j])
        store(Y, q, j, copy(queue, T.yb[:, c:c + PW], T.ow[:, w:w + 512].indirect(T.offo[:, 4 * i:4 * i + 4])))

    def own_picks():
        after(V, k5)
        for j in range(2):
            list_of(r, j, 2 * NC + j)
        for j in range(2):
            pick(A, r, j)

    def choices():
        at, rd = bank()
        after(P, q4).wait_ge(S.sma, 2 * count * (NR - 1))
        for q in range(NR):
            s = PG * (NR if q == r else 1 + slot(q, r))
            mm = P.matmul_mx(T.ps[:, at:at + 128], T.hq4[:, 10 - 2 * q:138 - 2 * q], T.hp4[:, 10 - 2 * q:138 - 2 * q],
                             T.sq[:, s:s + 128], T.sp[:, s:s + 128], q == 0, q == NR - 1)
        v2, v4, v5 = lowest_best(1, T.ps[:, at:at + 8], T.ps[:, at:at + 1], done(mm))
        rd.append(v2)
        after(Y, v4)
        for j in range(2):
            Y.dma_start(T.ch[j:j + 1, :], T.bb[j:2 * NR:2, 79:80]).then_inc(S.yst, 16)
            stores[0] += 16
        after(V, v5)
        for q in whole:
            for j in range(2):
                list_of(q, j, 32 + 2 * q + j)

    def part(name, a, b, queues):
        for u, q in enumerate(whole):
            P.wait_ge(S[name % q], 2 * count)
            for j in range(2):
                w = 1024 * (1 + u) + 512 * j
                product = times_queries(j, T["eq"], T["ep"], 512 * u + a, 512 * u + b)
                ready.setdefault((q, j), []).append(take(queues[2 * u + j], T.ow[:, w + a:w + b], product, 0, b - a))

    def picks():
        for q in whole:
            pick(V, q, 0)
            pick(A, q, 1)

    def arrived(t):
        P.wait_ge(S["pa%d" % t], 2 * count)
        q = chosen[t]
        for j, queue in enumerate((V, A)):
            c = PW * (j * NR + q)
            sem = take(queue, T.yb[:, c:c + PW], times_queries(j, T.lq, T.lp, 128 * t, 128 * t + 128), PW * j, PW * j + PW)
            store(A if (t, j) == (NC - 1, 1) else Y, q, j, sem)

    own_picks()
    part("e1_%d", cut, 512, (A, A, V, A))
    choices()
    arrived(0)
    part("e0_%d", 0, cut, (V, A, V, A))
    picks()
    arrived(1)
    arrived(2)

    g.wait_ge(S.left, sent[0])
    Y.wait_ge(S.yst, stores[0])
